import numpy as np
import ml_dtypes


def mxq(x, axis, fmt="e4m3"):
    dtype, down = {"e4m3": (ml_dtypes.float8_e4m3fn, 7), "e5m2": (ml_dtypes.float8_e5m2, 14)}[fmt]
    v = np.moveaxis(np.asarray(x, np.float32).astype(ml_dtypes.bfloat16).astype(np.float64), axis, -1)
    blocks = v.reshape(v.shape[:-1] + (-1, 32))
    amax = np.abs(blocks).max(-1, keepdims=True)
    byte = np.maximum(np.where(amax > 0, np.frexp(amax)[1] - 1 + 127, 0) - down, 1)
    scale = np.exp2(byte - 127.0)
    codes = (blocks / scale).astype(np.float32).astype(dtype).astype(np.float64)
    return np.moveaxis((codes * scale).reshape(v.shape), -1, axis)


WIDE = False


def mx_kscale(k):
    if not WIDE:
        return np.ones(k)
    levels = np.array([10, -10, 5, -5, 0])
    if k % 512:
        return np.exp2(np.random.permutation(np.resize(levels, k // 32))).repeat(32)
    a = np.empty((k // 512, 16))
    for p in range(k // 512):
        a[p, :8] = np.random.permutation(np.resize(levels, 8))
        for g in range(8):
            far = levels[np.abs(levels - a[p, g]) >= 10]
            a[p, g + 8] = far[np.random.randint(len(far))]
    return np.exp2(a.ravel()).repeat(32)


def f64(x):
    return np.asarray(x).astype(np.float64)


def striped(idx):
    return np.tile(idx.reshape(-1, 16).T, (8, 1)).astype(np.uint16)


def unstriped(offs):
    return offs[:16].T.reshape(-1).astype(np.int64)


E2M1 = np.array([0.0, 0.5, 1.0, 1.5, 2.0, 3.0, 4.0, 6.0, -0.0, -0.5, -1.0, -1.5, -2.0, -3.0, -4.0, -6.0])


def pack_weight(w, fmt):
    k, n = w.shape
    w = f64(np.asarray(w, np.float32).astype(ml_dtypes.bfloat16)).reshape(k // 32, 32, n)
    amax = np.abs(w).max(1)
    if fmt == "e4m3":
        byte = np.frexp(amax)[1] - 1 + 127 - 7
    else:
        mant, ex = np.frexp(amax / 6.0)
        byte = np.where(mant > 0.5, ex, ex - 1) + 127
    byte = np.clip(np.where(amax > 0, byte, 1), 1, 254)
    scaled = (w * np.exp2(127.0 - byte)[:, None, :]).reshape(k, n).astype(np.float32)
    by_word = np.ascontiguousarray(scaled.reshape(k // 512, 128, 4, n).transpose(0, 1, 3, 2))
    if fmt == "e4m3":
        words = by_word.astype(ml_dtypes.float8_e4m3fn).view(np.uint8)
    else:
        c = by_word.astype(ml_dtypes.float4_e2m1fn).view(np.uint8) & 0xF
        words = (c[..., 0::2] | (c[..., 1::2] << 4)).reshape(k // 512, 128, 2 * n)
    return np.ascontiguousarray(words), np.ascontiguousarray(byte.astype(np.uint8).reshape(k // 512, 16, n))


def unpack_weight(words, scales, fmt):
    g, _, n = scales.shape
    words = np.ascontiguousarray(words).reshape(g, 128, n, -1)
    if fmt == "e4m3":
        vals = words.view(ml_dtypes.float8_e4m3fn).astype(np.float64)
    else:
        nib = np.empty((g, 128, n, 4), np.uint8)
        nib[..., 0::2] = words & 0xF
        nib[..., 1::2] = words >> 4
        vals = E2M1[nib]
    vals = vals * np.repeat(np.exp2(scales.astype(np.float64) - 127.0), 8, axis=1)[..., None]
    return vals.transpose(0, 1, 3, 2).reshape(g * 512, n)


def gelu(v):
    return 0.5 * v * (1.0 + np.tanh(np.sqrt(2.0 / np.pi) * (v + 0.044715 * v**3)))


def bf(x):
    return np.asarray(x, np.float32).astype(ml_dtypes.bfloat16)


def planes(Y):
    n, m = Y.shape
    b = f64(bf(Y)).reshape(n // 32, 32, m)
    amax = np.abs(b).max(1)
    byte = np.clip(np.where(amax > 0, np.frexp(amax)[1] - 1 + 127 - 7, 1), 1, 254)
    codes = (b * np.exp2(127.0 - byte)[:, None, :]).reshape(n, m).astype(np.float32).astype(ml_dtypes.float8_e4m3fn).view(np.uint8)
    words = codes.reshape(n // 512, 128, 4, m).transpose(0, 1, 3, 2)
    return np.ascontiguousarray(words), np.ascontiguousarray(byte.astype(np.uint8).reshape(n // 512, 16, m))


K, H, N, T, S, T2, P = 1024, 1024, 512, 4096, 1024, 2048, 1024

def setup_inputs():
    n = np.random.standard_normal
    s = mx_kscale(K)[:, None]
    u = mx_kscale(H)[:, None]
    d = {}
    d["tab_words"], d["tab_scales"] = pack_weight(n((K, T)) * s, "e4m3")
    d["w1"] = (2.0 * n((K, H)) / K**0.5 / s).astype(np.float32)
    d["w4_words"], d["w4_scales"] = pack_weight(2.0 * n((K, H)) / K**0.5 / s, "e2m1")
    d["gain"] = (0.45 * np.exp(0.3 * n(H)) * u[:, 0]).astype(np.float32)
    d["page0"] = (n((H, T2)) * u).astype(np.float32)
    d["wgs"] = np.exp(0.3 * n((128, S))).astype(np.float32)
    d["vec"] = np.exp(0.4 * n(H)).astype(np.float32)
    d["w2"] = (n((H, N)) / H**0.5 / u).astype(np.float32)
    d["offs"] = striped(np.random.permutation(T)[:S])
    d["offs2"] = striped(np.random.permutation(T2)[:S])
    d["offs3"] = striped(np.random.permutation(T2)[:P])
    return d

def reference(tab_words, tab_scales, w1, w4_words, w4_scales, gain, page0, wgs, vec, w2, offs, offs2, offs3):
    v = unpack_weight(tab_words, tab_scales, "e4m3")[:, unstriped(offs)]
    w4 = unpack_weight(w4_words, w4_scales, "e2m1")
    along = mxq(f64(w1), 0, "e4m3").T @ v
    across = w4.T @ v
    h = np.sqrt(1.0 + (along * along + across * across)) * f64(gain)[:, None]
    page = f64(page0).copy()
    page[:, unstriped(offs2)] = np.tile(f64(wgs), (H // 128, 1)) * h
    x = page[:, unstriped(offs3)] * f64(vec)[:, None]
    y = mxq(f64(w2), 0, "e4m3").T @ mxq(x, 0, "e4m3")
    words, scales = planes(page)
    return y, page, words, scales

@@ -1,0 +1,333 @@
+from contextlib import ExitStack
+
+import concourse.mybir as mybir
+from concourse.masks import make_identity
+
+K, H, N, T, S, T2, PICK = 1024, 1024, 512, 4096, 1024, 2048, 1024
+FLOPS = 2 * (2 * K * H * S + H * N * PICK)
+
+F32 = mybir.dt.float32
+BF16 = mybir.dt.bfloat16
+I32 = mybir.dt.int32
+U32 = mybir.dt.uint32
+U16 = mybir.dt.uint16
+U8 = mybir.dt.uint8
+FP8X4 = mybir.dt.float8_e4m3fn_x4
+FP4X4 = mybir.dt.float4_e2m1fn_x4
+ACT = mybir.ActivationFunctionType
+MULT = mybir.AluOpType.mult
+
+P = 128
+PACK = 4
+PASS = P * PACK
+BANK = 512
+LANES = 16
+
+
+def tile_list_plate_thinning_features_kernel(
+    tc, tab_words, tab_scales, w1, w4_words, w4_scales, gain, page0, wgs, vec, w2, offs, offs2, offs3,
+    out_0, out_1, out_2, out_3,
+):
+    nc = tc.nc
+    with ExitStack() as ctx:
+        held = ctx.enter_context(tc.tile_pool(name="held", bufs=1))
+        big = ctx.enter_context(tc.tile_pool(name="big", bufs=1))
+        raw = ctx.enter_context(tc.tile_pool(name="raw", bufs=4))
+        pages = ctx.enter_context(tc.tile_pool(name="pages", bufs=7))
+        woven = ctx.enter_context(tc.tile_pool(name="woven", bufs=4))
+        small = ctx.enter_context(tc.tile_pool(name="small", bufs=6))
+        planes = ctx.enter_context(tc.tile_pool(name="planes", bufs=4))
+        psum = ctx.enter_context(tc.psum_pool(name="psum", bufs=8))
+
+        def entries(lst, lo, hi):
+            return lst[:, lo // LANES : hi // LANES]
+
+        def weave(copy, src, late=None):
+            if late is None:
+                dst = woven.tile([P, BANK, PACK], BF16, name="woven", align_bytes=64)
+            else:
+                dst = held.tile([P, BANK, PACK], BF16, name="woven_late", tag="late%d" % late, align_bytes=64)
+            copy(out=dst[:].rearrange("p (c i) t -> p c t i", i=4), in_=src.rearrange("p t (c i) -> p c t i", i=4))
+            return dst
+
+        def quantise(codes, scales, src):
+            nc.vector.quantize_mx(out=codes.bitcast(FP8X4), scales=scales, in_=src[:].rearrange("p c t -> p (c t)"))
+
+        list_tab = held.tile([P, S // LANES], U16, name="list_tab")
+        list_put = held.tile([P, S // LANES], U16, name="list_put")
+        list_get = held.tile([P, PICK // LANES], U16, name="list_get")
+        ident = held.tile([P, P], F32, name="ident")
+        gain_sb = held.tile([P, 2, PACK], F32, name="gain_sb")
+        warm = held.tile([P, 8], F32, name="warm")
+        w4_codes = held.tile([P, 2, 2 * H], U8, name="w4_codes", tag="late2", align_bytes=64)
+        w4_sc = held.tile([P, 2, H], U8, name="w4_sc", align_bytes=64)
+        v_codes = [held.tile([P, S], U32, name="v_codes", tag="late%d" % a, align_bytes=64) for a in range(2)]
+        v_sc = [held.tile([P, S], U8, name="v_sc", tag="v_sc%d" % a, align_bytes=64) for a in range(2)]
+        w1_pair = [held.tile([P, 2, BANK], U32, name="w1_codes", tag="late%d" % (4 - g), align_bytes=64) for g in range(2)]
+        w1_codes = [[w1_pair[g][:, a, :] for a in range(2)] for g in range(2)]
+        w1_sc = [[held.tile([P, BANK], U8, name="w1_sc%d%d" % (g, a), align_bytes=64) for a in range(2)] for g in range(2)]
+        w2_codes = [held.tile([P, N], U32, name="w2_codes%d" % g, align_bytes=64) for g in range(2)]
+        w2_sc = [held.tile([P, N], U8, name="w2_sc%d" % g, align_bytes=64) for g in range(2)]
+        x_codes = [[held.tile([P, BANK], U32, name="x_codes%d%d" % (g, u), align_bytes=64) for u in range(2)] for g in range(2)]
+        x_sc = [[held.tile([P, BANK], U8, name="x_sc%d%d" % (g, u), align_bytes=64) for u in range(2)] for g in range(2)]
+        page_sc = [held.tile([P, T2], U8, name="page_sc%d" % g, align_bytes=64) for g in range(2)]
+        wgs_sb = [held.tile([P, PACK, BANK], F32, name="wgs_sb%d" % u) for u in range(2)]
+
+        def load_rows(w, g_rows, cols):
+            dst = raw.tile([P, PACK, BANK], F32, name="raw", tag="raw")
+            nc.sync.dma_start(out=dst[:], in_=w[g_rows * PASS : (g_rows + 1) * PASS, cols].rearrange("(p i) c -> p i c", i=PACK))
+            return dst
+
+        page0_rows = page0.rearrange("(g p t) m -> g t p m", g=2, t=PACK)
+        out1_rows = out_1.rearrange("(g p t) m -> g t p m", g=2, t=PACK)
+        page = {}
+
+        def load_page(g, t):
+            page[g, t] = pages.tile([P, T2], F32, name="page")
+            nc.sync.dma_start(out=page[g, t][:], in_=page0_rows[g, t])
+
+        tab_sc = raw.tile([P, 2, T], U8, name="tab_sc", tag="raw")
+        nc.vector.memset(tab_sc[:].rearrange("p a t -> p (a t)").bitcast(I32), 0)
+        nc.gpsimd.memset(w4_sc[:].rearrange("p a t -> p (a t)").bitcast(I32), 0)
+        nc.vector.memset(warm[:], 1.0)
+        nc.scalar.activation(out=warm[:, 4:5], in_=warm[:, 0:1], func=ACT.Sqrt)
+
+        make_identity(nc, ident[:])
+        def load_table(a):
+            words = big.tile([P, T], I32, name="tab", tag="big%d" % a)
+            nc.sync.dma_start(out=words[:], in_=tab_words[a].rearrange("p t i -> p (t i)").bitcast(I32))
+            return words
+
+        def load_w4(g):
+            cols = slice(2 * g * PASS, 2 * (g + 1) * PASS)
+            nc.sync.dma_start(out=w4_codes[:, :, cols].bitcast(I32), in_=w4_words.rearrange("a p c -> p a c")[:, :, cols].bitcast(I32))
+
+        def load_wgs(u):
+            rows = wgs.rearrange("(b t) j -> b t j", t=PACK)[:, :, u * BANK : (u + 1) * BANK]
+            for q in range(4):
+                nc.sync.dma_start(out=wgs_sb[u][32 * q : 32 * q + 32, :, :], in_=rows)
+
+        nc.sync.dma_start(out=list_tab[:], in_=offs)
+        w1_raw = [load_rows(w1, a, slice(0, PASS)) for a in range(2)]
+        for q in range(4):
+            nc.sync.dma_start(
+                out=tab_sc[32 * q : 32 * q + 4, :, :].bitcast(I32),
+                in_=tab_scales[:, 4 * q : 4 * q + 4, :].rearrange("a r t -> r a t").bitcast(I32),
+            )
+        nc.sync.dma_start(out=gain_sb[:], in_=gain.rearrange("(g p t) -> p g t", g=2, t=PACK))
+        tab = [load_table(0)]
+        for q in range(4):
+            nc.sync.dma_start(
+                out=w4_sc[32 * q : 32 * q + 4, :, :].bitcast(I32),
+                in_=w4_scales[:, 4 * q : 4 * q + 4, :].rearrange("a r c -> r a c").bitcast(I32),
+            )
+        nc.sync.dma_start(out=list_put[:], in_=offs2)
+        load_w4(0)
+        tab.append(load_table(1))
+        load_wgs(0)
+        for t in range(4):
+            load_page(0, t)
+        load_wgs(1)
+        w1_raw_late = [load_rows(w1, a, slice(PASS, 2 * PASS)) for a in range(2)]
+        load_w4(1)
+        nc.sync.dma_start(out=list_get[:], in_=offs3)
+        w2_raw = [load_rows(w2, g, slice(0, N)) for g in range(2)]
+        for t in range(3):
+            load_page(1, t)
+
+        def gather_scales(a, lo, hi):
+            nc.vector.tensor_copy(out=v_sc[a][:, lo:hi], in_=tab_sc[:, a, :].indirect(entries(list_tab, lo, hi)))
+
+        def gather_words(a, lo, hi):
+            nc.vector.tensor_copy(out=v_codes[a][:, lo:hi], in_=tab[a][:].bitcast(U32).indirect(entries(list_tab, lo, hi)))
+
+        for a in range(2):
+            grouped = weave(nc.scalar.copy, w1_raw[a][:])
+            gather_scales(a, 0, S)
+            quantise(w1_codes[0][a], w1_sc[0][a][:], grouped)
+        gather_words(0, 0, S)
+        gather_words(1, 0, S // 2)
+        gather_words(1, S // 2, S)
+
+        h = {}
+
+        def products(g, c):
+            cols = slice(c * P, (c + 1) * P)
+            across = psum.tile([P, BANK], F32, name="bank")
+            along = psum.tile([P, BANK], F32, name="bank")
+            for a in range(2):
+                nc.tensor.matmul_mx(
+                    out=across[:], lhsT=v_codes[a][:, cols].bitcast(FP8X4), lhsT_scale=v_sc[a][:, cols],
+                    rhs=w4_codes[:, a, 2 * g * PASS : 2 * (g + 1) * PASS].bitcast(FP4X4),
+                    rhs_scale=w4_sc[:, a, g * PASS : (g + 1) * PASS], start=(a == 0), stop=(a == 1),
+                )
+            for a in range(2):
+                nc.tensor.matmul_mx(
+                    out=along[:], lhsT=v_codes[a][:, cols].bitcast(FP8X4), lhsT_scale=v_sc[a][:, cols],
+                    rhs=w1_codes[g][a].bitcast(FP8X4), rhs_scale=w1_sc[g][a][:], start=(a == 0), stop=(a == 1),
+                )
+            squares = []
+            for bank in (across, along):
+                sq = small.tile([P, PACK, P], F32, name="small")
+                nc.scalar.activation(out=sq[:], in_=bank[:].rearrange("j (p t) -> j t p", t=PACK), func=ACT.Square)
+                squares.append(sq)
+            return squares
+
+        def magnitude(g, c, squares):
+            total = psum.tile([P, PACK, P], F32, name="bank")
+            for t in range(PACK):
+                for n, sq in enumerate(squares):
+                    nc.tensor.matmul(out=total[:, t, :], lhsT=sq[:, t, :], rhs=ident[:], is_transpose=True, start=(n == 0), stop=(n == 1))
+            nc.scalar.activation(out=h[g][:, :, c * P : (c + 1) * P], in_=total[:], func=ACT.Sqrt, bias=1.0)
+
+        def apply_gain(g, t, lo, hi):
+            nc.scalar.activation(out=h[g][:, t, lo:hi], in_=h[g][:, t, lo:hi], func=ACT.Copy, scale=gain_sb[:, g, t : t + 1])
+
+        def put(g, t, lo, hi):
+            nc.vector.tensor_tensor(
+                out=page[g, t][:].indirect(entries(list_put, lo, hi)), in0=h[g][:, t, lo:hi], in1=wgs_sb[lo // BANK][:, t, lo % BANK : lo % BANK + hi - lo], op=MULT
+            )
+
+        def store_page(g, t):
+            nc.sync.dma_start(out=out1_rows[g, t], in_=page[g, t][:])
+
+        picked = {}
+
+        def get(g, t, lo, hi):
+            nc.vector.tensor_copy(out=picked[g][:, t, lo:hi], in_=page[g, t][:].indirect(entries(list_get, lo, hi)))
+
+        def apply_vec(g, t, lo, hi):
+            nc.scalar.activation(out=picked[g][:, t, lo:hi], in_=picked[g][:, t, lo:hi], func=ACT.Copy, scale=vec_sb[:, g, t : t + 1])
+
+        def stage_one(g, after):
+            h[g] = big.tile([P, PACK, S], F32, name="h", tag=("big2", "big0")[g])
+            pending = products(g, 0)
+            for c in range(S // P):
+                ahead = products(g, c + 1) if c + 1 < S // P else None
+                magnitude(g, c, pending)
+                pending = ahead
+                for step in after.get(c, ()):
+                    step()
+
+        def gain_put(g, t, lo, hi):
+            def step():
+                apply_gain(g, t, lo, hi)
+                for start in range(lo, hi, BANK):
+                    put(g, t, start, min(hi, start + BANK))
+            return step
+
+        staged = {}
+
+        def stage_page(g, t, chunks):
+            for c in chunks:
+                if (g, c) not in staged:
+                    staged[g, c] = raw.tile([P, PACK, BANK], F32, name="staged", tag="raw")
+                nc.sync.dma_start(out=staged[g, c][:, t, :], in_=page[g, t][:, c * BANK : (c + 1) * BANK])
+
+        def plane_chunk(g, c, grouped):
+            codes = planes.tile([P, BANK], U32, name="page_codes", align_bytes=64)
+            quantise(codes[:], page_sc[g][:, c * BANK : (c + 1) * BANK], grouped)
+            nc.sync.dma_start(
+                out=out_2[g].rearrange("p m t -> p (m t)")[:, c * BANK * PACK : (c + 1) * BANK * PACK].bitcast(I32),
+                in_=codes[:].bitcast(I32),
+            )
+
+        def store_plane_scales(g):
+            for q in range(4):
+                nc.sync.dma_start(out=out_3[g, 4 * q : 4 * q + 4, :].bitcast(I32), in_=page_sc[g][32 * q : 32 * q + 4, :].bitcast(I32))
+
+        def weave_x(copy, g, u):
+            return weave(copy, picked[g][:, :, u * BANK : (u + 1) * BANK])
+
+        def late_w1(a):
+            def step():
+                quantise(w1_codes[1][a], w1_sc[1][a][:], weave(nc.scalar.copy, w1_raw_late[a][:]))
+            return step
+
+        Q, HALF = S // 4, S // 2
+        stage_one(0, {
+            1: [gain_put(0, t, 0, Q) for t in range(3)],
+            3: [gain_put(0, t, Q, HALF) for t in range(3)] + [gain_put(0, 3, 0, HALF)],
+            5: [gain_put(0, 0, HALF, 3 * Q)],
+            7: [gain_put(0, 0, 3 * Q, S), late_w1(0), gain_put(0, 1, HALF, S), late_w1(1)],
+        })
+        picked[0] = big.tile([P, PACK, PICK], F32, name="picked", tag="big1")
+        for t in range(4):
+            if t > 1:
+                gain_put(0, t, HALF, S)()
+        for g in range(2):
+            quantise(w2_codes[g][:], w2_sc[g][:], weave(nc.scalar.copy, w2_raw[g][:]))
+        for t in range(4):
+            stage_page(0, t, range(4))
+            store_page(0, t)
+            get(0, t, 0, PICK)
+        load_page(1, 3)
+        stage_one(1, {3: [gain_put(1, 0, 0, HALF), gain_put(1, 1, 0, HALF)], 7: [gain_put(1, 0, HALF, S), gain_put(1, 1, HALF, S)]})
+        vec_sb = held.tile([P, 2, PACK], F32, name="vec_sb", tag="v_sc0", align_bytes=64)
+        nc.sync.dma_start(out=vec_sb[:], in_=vec.rearrange("(g p t) -> p g t", g=2, t=PACK))
+        picked[1] = big.tile([P, PACK, PICK], F32, name="picked", tag="big2")
+        for t in range(2):
+            get(1, t, 0, PICK)
+            store_page(1, t)
+        for c in range(4):
+            plane_chunk(0, c, weave(nc.scalar.copy, staged[0, c][:], late=c))
+        store_plane_scales(0)
+        gain_put(1, 2, 0, S)()
+        for t in range(2):
+            stage_page(1, t, range(4))
+        get(1, 2, 0, PICK)
+        store_page(1, 2)
+        stage_page(1, 2, range(4))
+        for t in range(4):
+            apply_vec(0, t, 0, PICK)
+        for u in range(2):
+            quantise(x_codes[0][u][:], x_sc[0][u][:], weave_x(nc.scalar.copy, 0, u))
+        gain_put(1, 3, 0, S)()
+        for t in range(3):
+            apply_vec(1, t, 0, PICK)
+
+        y = {}
+
+        def y_pass(g, u):
+            for n in range(N // P):
+                if g == 0:
+                    y[n, u] = psum.tile([P, BANK], F32, name="bank")
+                cols = slice(n * P, (n + 1) * P)
+                nc.tensor.matmul_mx(
+                    out=y[n, u][:], lhsT=w2_codes[g][:, cols].bitcast(FP8X4), lhsT_scale=w2_sc[g][:, cols],
+                    rhs=x_codes[g][u][:].bitcast(FP8X4), rhs_scale=x_sc[g][u][:], start=(g == 0), stop=(g == 1),
+                )
+
+        def y_out(copy, n, u):
+            res = small.tile([P, BANK], F32, name="small")
+            copy(out=res[:], in_=y[n, u][:])
+            nc.sync.dma_start(out=out_0[n * P : (n + 1) * P, u * BANK : (u + 1) * BANK], in_=res[:])
+
+        for u in range(2):
+            y_pass(0, u)
+
+        stage_page(1, 3, range(4))
+        store_page(1, 3)
+        get(1, 3, 0, HALF)
+        get(1, 3, HALF, PICK)
+        x_woven = []
+        for u in range(2):
+            apply_vec(1, 3, u * HALF, (u + 1) * HALF)
+            x_woven.append(weave_x(nc.scalar.copy, 1, u))
+        first = weave(nc.vector.tensor_copy, staged[1, 0][:])
+        second = weave(nc.vector.tensor_copy, staged[1, 1][:])
+        quantise(x_codes[1][0][:], x_sc[1][0][:], x_woven[0])
+        y_pass(1, 0)
+        plane_chunk(1, 0, first)
+        plane_chunk(1, 1, second)
+        third = weave(nc.vector.tensor_copy, staged[1, 2][:])
+        quantise(x_codes[1][1][:], x_sc[1][1][:], x_woven[1])
+        y_pass(1, 1)
+        fourth = weave(nc.vector.tensor_copy, staged[1, 3][:])
+        for n in range(N // P):
+            y_out(nc.scalar.copy, n, 0)
+        plane_chunk(1, 2, third)
+        plane_chunk(1, 3, fourth)
+        store_plane_scales(1)
+        for n in range(N // P):
+            y_out(nc.scalar.copy if n % 2 == 0 else nc.vector.tensor_copy, n, 1)

@@ -33,20 +33,16 @@ def tile_list_plate_thinning_features_kernel(
         held = ctx.enter_context(tc.tile_pool(name="held", bufs=1))
         big = ctx.enter_context(tc.tile_pool(name="big", bufs=1))
         raw = ctx.enter_context(tc.tile_pool(name="raw", bufs=4))
-        pages = ctx.enter_context(tc.tile_pool(name="pages", bufs=7))
-        woven = ctx.enter_context(tc.tile_pool(name="woven", bufs=4))
-        small = ctx.enter_context(tc.tile_pool(name="small", bufs=6))
+        pages = ctx.enter_context(tc.tile_pool(name="pages", bufs=8))
+        small = ctx.enter_context(tc.tile_pool(name="small", bufs=5))
         planes = ctx.enter_context(tc.tile_pool(name="planes", bufs=4))
         psum = ctx.enter_context(tc.psum_pool(name="psum", bufs=8))
 
         def entries(lst, lo, hi):
             return lst[:, lo // LANES : hi // LANES]
 
-        def weave(copy, src, late=None):
-            if late is None:
-                dst = woven.tile([P, BANK, PACK], BF16, name="woven", align_bytes=64)
-            else:
-                dst = held.tile([P, BANK, PACK], BF16, name="woven_late", tag="late%d" % late, align_bytes=64)
+        def weave(copy, src, slot):
+            dst = held.tile([P, BANK, PACK], BF16, name="woven", tag="slot%d" % slot, align_bytes=64)
             copy(out=dst[:].rearrange("p (c i) t -> p c t i", i=4), in_=src.rearrange("p t (c i) -> p c t i", i=4))
             return dst
 
@@ -59,11 +55,11 @@ def tile_list_plate_thinning_features_kernel(
         ident = held.tile([P, P], F32, name="ident")
         gain_sb = held.tile([P, 2, PACK], F32, name="gain_sb")
         warm = held.tile([P, 8], F32, name="warm")
-        w4_codes = held.tile([P, 2, 2 * H], U8, name="w4_codes", tag="late2", align_bytes=64)
+        w4_codes = held.tile([P, 2, 2, 2 * PASS], U8, name="w4_codes", tag="slot2", align_bytes=64)
         w4_sc = held.tile([P, 2, H], U8, name="w4_sc", align_bytes=64)
-        v_codes = [held.tile([P, S], U32, name="v_codes", tag="late%d" % a, align_bytes=64) for a in range(2)]
+        v_codes = [held.tile([P, S], U32, name="v_codes", tag="slot%d" % a, align_bytes=64) for a in range(2)]
         v_sc = [held.tile([P, S], U8, name="v_sc", tag="v_sc%d" % a, align_bytes=64) for a in range(2)]
-        w1_pair = [held.tile([P, 2, BANK], U32, name="w1_codes", tag="late%d" % (4 - g), align_bytes=64) for g in range(2)]
+        w1_pair = [held.tile([P, 2, BANK], U32, name="w1_codes", tag="slot%d" % (4 - g), align_bytes=64) for g in range(2)]
         w1_codes = [[w1_pair[g][:, a, :] for a in range(2)] for g in range(2)]
         w1_sc = [[held.tile([P, BANK], U8, name="w1_sc%d%d" % (g, a), align_bytes=64) for a in range(2)] for g in range(2)]
         w2_codes = [held.tile([P, N], U32, name="w2_codes%d" % g, align_bytes=64) for g in range(2)]
@@ -100,7 +96,7 @@ def tile_list_plate_thinning_features_kernel(
 
         def load_w4(g):
             cols = slice(2 * g * PASS, 2 * (g + 1) * PASS)
-            nc.sync.dma_start(out=w4_codes[:, :, cols].bitcast(I32), in_=w4_words.rearrange("a p c -> p a c")[:, :, cols].bitcast(I32))
+            nc.sync.dma_start(out=w4_codes[:, g, :, :].bitcast(I32), in_=w4_words.rearrange("a p c -> p a c")[:, :, cols].bitcast(I32))
 
         def load_wgs(u):
             rows = wgs.rearrange("(b t) j -> b t j", t=PACK)[:, :, u * BANK : (u + 1) * BANK]
@@ -132,7 +128,7 @@ def tile_list_plate_thinning_features_kernel(
         load_w4(1)
         nc.sync.dma_start(out=list_get[:], in_=offs3)
         w2_raw = [load_rows(w2, g, slice(0, N)) for g in range(2)]
-        for t in range(3):
+        for t in range(4):
             load_page(1, t)
 
         def gather_scales(a, lo, hi):
@@ -142,7 +138,7 @@ def tile_list_plate_thinning_features_kernel(
             nc.vector.tensor_copy(out=v_codes[a][:, lo:hi], in_=tab[a][:].bitcast(U32).indirect(entries(list_tab, lo, hi)))
 
         for a in range(2):
-            grouped = weave(nc.scalar.copy, w1_raw[a][:])
+            grouped = weave(nc.scalar.copy, w1_raw[a][:], 5 + a)
             gather_scales(a, 0, S)
             quantise(w1_codes[0][a], w1_sc[0][a][:], grouped)
         gather_words(0, 0, S)
@@ -150,6 +146,11 @@ def tile_list_plate_thinning_features_kernel(
         gather_words(1, S // 2, S)
 
         h = {}
+        edges = ((0, S // 4, S // 2, S), (0, S // 2, S))
+
+        def h_piece(g, lo, hi):
+            first, last = max(e for e in edges[g] if e <= lo), min(e for e in edges[g] if e >= hi)
+            return h[g][:, PACK * first : PACK * last].rearrange("p (t j) -> p t j", t=PACK)[:, :, lo - first : hi - first]
 
         def products(g, c):
             cols = slice(c * P, (c + 1) * P)
@@ -158,7 +159,7 @@ def tile_list_plate_thinning_features_kernel(
             for a in range(2):
                 nc.tensor.matmul_mx(
                     out=across[:], lhsT=v_codes[a][:, cols].bitcast(FP8X4), lhsT_scale=v_sc[a][:, cols],
-                    rhs=w4_codes[:, a, 2 * g * PASS : 2 * (g + 1) * PASS].bitcast(FP4X4),
+                    rhs=w4_codes[:, g, a, :].bitcast(FP4X4),
                     rhs_scale=w4_sc[:, a, g * PASS : (g + 1) * PASS], start=(a == 0), stop=(a == 1),
                 )
             for a in range(2):
@@ -178,15 +179,33 @@ def tile_list_plate_thinning_features_kernel(
             for t in range(PACK):
                 for n, sq in enumerate(squares):
                     nc.tensor.matmul(out=total[:, t, :], lhsT=sq[:, t, :], rhs=ident[:], is_transpose=True, start=(n == 0), stop=(n == 1))
-            nc.scalar.activation(out=h[g][:, :, c * P : (c + 1) * P], in_=total[:], func=ACT.Sqrt, bias=1.0)
+            nc.scalar.activation(out=h_piece(g, c * P, (c + 1) * P), in_=total[:], func=ACT.Sqrt, bias=1.0)
 
-        def apply_gain(g, t, lo, hi):
-            nc.scalar.activation(out=h[g][:, t, lo:hi], in_=h[g][:, t, lo:hi], func=ACT.Copy, scale=gain_sb[:, g, t : t + 1])
-
-        def put(g, t, lo, hi):
+        def put(g, t, lo, hi, values):
             nc.vector.tensor_tensor(
-                out=page[g, t][:].indirect(entries(list_put, lo, hi)), in0=h[g][:, t, lo:hi], in1=wgs_sb[lo // BANK][:, t, lo % BANK : lo % BANK + hi - lo], op=MULT
+                out=page[g, t][:].indirect(entries(list_put, lo, hi)), in0=values,
+                in1=wgs_sb[lo // BANK][:, t, lo % BANK : lo % BANK + hi - lo], op=MULT,
             )
+
+        def gain_put(g, t, lo, hi, dst=None):
+            def step():
+                src = h_piece(g, lo, hi)[:, t, :]
+                out = src if dst is None else dst()
+                nc.scalar.activation(out=out, in_=src, func=ACT.Copy, scale=gain_sb[:, g, t : t + 1])
+                put(g, t, lo, hi, out)
+            return step
+
+        def gained_tile(slot):
+            return held.tile([P, 2, BANK], F32, name="gained", tag="slot%d" % slot, align_bytes=64)
+
+        def gain_put_late(t, slot):
+            out = gained_tile(slot)
+            nc.vector.tensor_scalar(
+                out=out[:], in0=h[1][:].rearrange("p (u t j) -> p u t j", u=2, t=PACK)[:, :, t, :],
+                scalar1=gain_sb[:, 1, t : t + 1], scalar2=None, op0=MULT,
+            )
+            for u in range(2):
+                put(1, t, u * BANK, (u + 1) * BANK, out[:, u, :])
 
         def store_page(g, t):
             nc.sync.dma_start(out=out1_rows[g, t], in_=page[g, t][:])
@@ -200,7 +219,7 @@ def tile_list_plate_thinning_features_kernel(
             nc.scalar.activation(out=picked[g][:, t, lo:hi], in_=picked[g][:, t, lo:hi], func=ACT.Copy, scale=vec_sb[:, g, t : t + 1])
 
         def stage_one(g, after):
-            h[g] = big.tile([P, PACK, S], F32, name="h", tag=("big2", "big0")[g])
+            h[g] = big.tile([P, PACK * S], F32, name="h", tag=("big2", "big0")[g])
             pending = products(g, 0)
             for c in range(S // P):
                 ahead = products(g, c + 1) if c + 1 < S // P else None
@@ -208,13 +227,6 @@ def tile_list_plate_thinning_features_kernel(
                 pending = ahead
                 for step in after.get(c, ()):
                     step()
-
-        def gain_put(g, t, lo, hi):
-            def step():
-                apply_gain(g, t, lo, hi)
-                for start in range(lo, hi, BANK):
-                    put(g, t, start, min(hi, start + BANK))
-            return step
 
         staged = {}
 
@@ -236,55 +248,70 @@ def tile_list_plate_thinning_features_kernel(
             for q in range(4):
                 nc.sync.dma_start(out=out_3[g, 4 * q : 4 * q + 4, :].bitcast(I32), in_=page_sc[g][32 * q : 32 * q + 4, :].bitcast(I32))
 
-        def weave_x(copy, g, u):
-            return weave(copy, picked[g][:, :, u * BANK : (u + 1) * BANK])
+        def weave_x(copy, g, u, slot):
+            return weave(copy, picked[g][:, :, u * BANK : (u + 1) * BANK], slot)
+
+        rounded = {}
+
+        def round_page(copy, t, c):
+            if c not in rounded:
+                rounded[c] = raw.tile([P, PACK, BANK], BF16, name="rounded", tag="raw")
+            copy(out=rounded[c][:, t, :], in_=page[1, t][:, c * BANK : (c + 1) * BANK])
 
         def late_w1(a):
             def step():
-                quantise(w1_codes[1][a], w1_sc[1][a][:], weave(nc.scalar.copy, w1_raw_late[a][:]))
+                quantise(w1_codes[1][a], w1_sc[1][a][:], weave(nc.scalar.copy, w1_raw_late[a][:], 5 + a))
+            return step
+
+        def late_w2(g):
+            def step():
+                quantise(w2_codes[g][:], w2_sc[g][:], weave(nc.scalar.copy, w2_raw[g][:], (4, 7)[g]))
             return step
 
         Q, HALF = S // 4, S // 2
         stage_one(0, {
             1: [gain_put(0, t, 0, Q) for t in range(3)],
-            3: [gain_put(0, t, Q, HALF) for t in range(3)] + [gain_put(0, 3, 0, HALF)],
-            5: [gain_put(0, 0, HALF, 3 * Q)],
-            7: [gain_put(0, 0, 3 * Q, S), late_w1(0), gain_put(0, 1, HALF, S), late_w1(1)],
+            3: [gain_put(0, t, Q, HALF) for t in range(3)] + [gain_put(0, 3, 0, Q), gain_put(0, 3, Q, HALF)],
+            7: [gain_put(0, 0, HALF, S), late_w1(0), late_w1(1)],
         })
+        pair = gained_tile(5)
+        gain_put(0, 1, HALF, S, lambda: pair[:, 0, :])()
+        gain_put(0, 2, HALF, S, lambda: pair[:, 1, :])()
+        gain_put(0, 3, HALF, S, lambda: gained_tile(6)[:, 0, :])()
         picked[0] = big.tile([P, PACK, PICK], F32, name="picked", tag="big1")
         for t in range(4):
-            if t > 1:
-                gain_put(0, t, HALF, S)()
-        for g in range(2):
-            quantise(w2_codes[g][:], w2_sc[g][:], weave(nc.scalar.copy, w2_raw[g][:]))
-        for t in range(4):
-            stage_page(0, t, range(4))
-            store_page(0, t)
             get(0, t, 0, PICK)
-        load_page(1, 3)
-        stage_one(1, {3: [gain_put(1, 0, 0, HALF), gain_put(1, 1, 0, HALF)], 7: [gain_put(1, 0, HALF, S), gain_put(1, 1, HALF, S)]})
+        stage_one(1, {
+            3: [gain_put(1, 0, 0, HALF), gain_put(1, 1, 0, HALF), late_w2(0), late_w2(1)],
+            7: [gain_put(1, 0, HALF, S), gain_put(1, 1, HALF, S)],
+        })
+        for c in range(4):
+            for t in range(4):
+                stage_page(0, t, [c])
         vec_sb = held.tile([P, 2, PACK], F32, name="vec_sb", tag="v_sc0", align_bytes=64)
         nc.sync.dma_start(out=vec_sb[:], in_=vec.rearrange("(g p t) -> p g t", g=2, t=PACK))
         picked[1] = big.tile([P, PACK, PICK], F32, name="picked", tag="big2")
         for t in range(2):
             get(1, t, 0, PICK)
-            store_page(1, t)
         for c in range(4):
-            plane_chunk(0, c, weave(nc.scalar.copy, staged[0, c][:], late=c))
+            plane_chunk(0, c, weave(nc.scalar.copy, staged[0, c][:], c))
         store_plane_scales(0)
-        gain_put(1, 2, 0, S)()
+        for t in range(4):
+            store_page(0, t)
+        gain_put_late(2, 3)
         for t in range(2):
-            stage_page(1, t, range(4))
-        get(1, 2, 0, PICK)
-        store_page(1, 2)
-        stage_page(1, 2, range(4))
+            store_page(1, t)
         for t in range(4):
             apply_vec(0, t, 0, PICK)
         for u in range(2):
-            quantise(x_codes[0][u][:], x_sc[0][u][:], weave_x(nc.scalar.copy, 0, u))
-        gain_put(1, 3, 0, S)()
+            quantise(x_codes[0][u][:], x_sc[0][u][:], weave_x(nc.scalar.copy, 0, u, 5 + u))
+        get(1, 2, 0, PICK)
+        store_page(1, 2)
+        gain_put_late(3, 6)
         for t in range(3):
             apply_vec(1, t, 0, PICK)
+            for c in range(4):
+                round_page(nc.scalar.copy, t, c)
 
         y = {}
 
@@ -298,36 +325,46 @@ def tile_list_plate_thinning_features_kernel(
                     rhs=x_codes[g][u][:].bitcast(FP8X4), rhs_scale=x_sc[g][u][:], start=(g == 0), stop=(g == 1),
                 )
 
+        out0_rows = out_0.rearrange("(n p) j -> p n j", p=P)
+        result = [pages.tile([P, N // P, BANK], F32, name="page") for u in range(2)]
+
         def y_out(copy, n, u):
-            res = small.tile([P, BANK], F32, name="small")
-            copy(out=res[:], in_=y[n, u][:])
-            nc.sync.dma_start(out=out_0[n * P : (n + 1) * P, u * BANK : (u + 1) * BANK], in_=res[:])
+            copy(out=result[u][:, n, :], in_=y[n, u][:])
+
+        def y_store(lo, hi, u):
+            nc.sync.dma_start(out=out0_rows[:, lo:hi, u * BANK : (u + 1) * BANK], in_=result[u][:, lo:hi, :])
 
         for u in range(2):
             y_pass(0, u)
 
-        stage_page(1, 3, range(4))
         store_page(1, 3)
         get(1, 3, 0, HALF)
         get(1, 3, HALF, PICK)
-        x_woven = []
-        for u in range(2):
-            apply_vec(1, 3, u * HALF, (u + 1) * HALF)
-            x_woven.append(weave_x(nc.scalar.copy, 1, u))
-        first = weave(nc.vector.tensor_copy, staged[1, 0][:])
-        second = weave(nc.vector.tensor_copy, staged[1, 1][:])
-        quantise(x_codes[1][0][:], x_sc[1][0][:], x_woven[0])
+        for c in (1, 2):
+            round_page(nc.scalar.copy, 3, c)
+        apply_vec(1, 3, 0, HALF)
+        x_first = weave_x(nc.scalar.copy, 1, 0, 4)
+        apply_vec(1, 3, HALF, PICK)
+        plane_chunk(1, 1, weave(nc.vector.tensor_copy, rounded[1][:], 1))
+        quantise(x_codes[1][0][:], x_sc[1][0][:], x_first)
         y_pass(1, 0)
-        plane_chunk(1, 0, first)
-        plane_chunk(1, 1, second)
-        third = weave(nc.vector.tensor_copy, staged[1, 2][:])
-        quantise(x_codes[1][1][:], x_sc[1][1][:], x_woven[1])
+        x_second = weave_x(nc.vector.tensor_copy, 1, 1, 7)
+        round_page(nc.scalar.copy, 3, 0)
+        first = weave(nc.scalar.copy, rounded[0][:], 0)
+        third = weave(nc.vector.tensor_copy, rounded[2][:], 4)
+        quantise(x_codes[1][1][:], x_sc[1][1][:], x_second)
         y_pass(1, 1)
-        fourth = weave(nc.vector.tensor_copy, staged[1, 3][:])
-        for n in range(N // P):
-            y_out(nc.scalar.copy, n, 0)
+        round_page(nc.vector.tensor_copy, 3, 3)
         plane_chunk(1, 2, third)
+        fourth = weave(nc.vector.tensor_copy, rounded[3][:], 3)
+        plane_chunk(1, 0, first)
         plane_chunk(1, 3, fourth)
         store_plane_scales(1)
         for n in range(N // P):
-            y_out(nc.scalar.copy if n % 2 == 0 else nc.vector.tensor_copy, n, 1)
+            y_out(nc.scalar.copy, n, 0)
+            if n % 2 == 1:
+                y_store(n - 1, n + 1, 0)
+        for n in range(N // P):
+            y_out(nc.scalar.copy if n < 2 else nc.vector.tensor_copy, n, 1)
+            if n % 2 == 1:
+                y_store(n - 1, n + 1, 1)

@@ -34,7 +34,7 @@ def tile_list_plate_thinning_features_kernel(
         big = ctx.enter_context(tc.tile_pool(name="big", bufs=1))
         raw = ctx.enter_context(tc.tile_pool(name="raw", bufs=4))
         pages = ctx.enter_context(tc.tile_pool(name="pages", bufs=8))
-        small = ctx.enter_context(tc.tile_pool(name="small", bufs=5))
+        small = ctx.enter_context(tc.tile_pool(name="small", bufs=4))
         planes = ctx.enter_context(tc.tile_pool(name="planes", bufs=4))
         psum = ctx.enter_context(tc.psum_pool(name="psum", bufs=8))
 
@@ -100,7 +100,7 @@ def tile_list_plate_thinning_features_kernel(
 
         def load_wgs(u):
             rows = wgs.rearrange("(b t) j -> b t j", t=PACK)[:, :, u * BANK : (u + 1) * BANK]
-            for q in range(4):
+            for q in (0, 2, 1, 3):
                 nc.sync.dma_start(out=wgs_sb[u][32 * q : 32 * q + 32, :, :], in_=rows)
 
         nc.sync.dma_start(out=list_tab[:], in_=offs)
@@ -162,7 +162,6 @@ def tile_list_plate_thinning_features_kernel(
                     rhs=w4_codes[:, g, a, :].bitcast(FP4X4),
                     rhs_scale=w4_sc[:, a, g * PASS : (g + 1) * PASS], start=(a == 0), stop=(a == 1),
                 )
-            for a in range(2):
                 nc.tensor.matmul_mx(
                     out=along[:], lhsT=v_codes[a][:, cols].bitcast(FP8X4), lhsT_scale=v_sc[a][:, cols],
                     rhs=w1_codes[g][a].bitcast(FP8X4), rhs_scale=w1_sc[g][a][:], start=(a == 0), stop=(a == 1),
@@ -181,11 +180,17 @@ def tile_list_plate_thinning_features_kernel(
                     nc.tensor.matmul(out=total[:, t, :], lhsT=sq[:, t, :], rhs=ident[:], is_transpose=True, start=(n == 0), stop=(n == 1))
             nc.scalar.activation(out=h_piece(g, c * P, (c + 1) * P), in_=total[:], func=ACT.Sqrt, bias=1.0)
 
-        def put(g, t, lo, hi, values):
-            nc.vector.tensor_tensor(
-                out=page[g, t][:].indirect(entries(list_put, lo, hi)), in0=values,
-                in1=wgs_sb[lo // BANK][:, t, lo % BANK : lo % BANK + hi - lo], op=MULT,
-            )
+        def put(g, t, lo, hi, values, factors=None):
+            if factors is None:
+                factors = wgs_sb[lo // BANK][:, t, lo % BANK : lo % BANK + hi - lo]
+            nc.vector.tensor_tensor(out=page[g, t][:].indirect(entries(list_put, lo, hi)), in0=values, in1=factors, op=MULT)
+
+        early = big.tile([P, PACK, BANK], F32, name="early", tag="big1")
+        for t in range(PACK):
+            nc.vector.tensor_scalar(out=early[:, t, :], in0=wgs_sb[0][:, t, :], scalar1=gain_sb[:, 0, t : t + 1], scalar2=None, op0=MULT)
+
+        def early_put(t, lo, hi):
+            return lambda: put(0, t, lo, hi, h_piece(0, lo, hi)[:, t, :], early[:, t, lo:hi])
 
         def gain_put(g, t, lo, hi, dst=None):
             def step():
@@ -208,7 +213,8 @@ def tile_list_plate_thinning_features_kernel(
                 put(1, t, u * BANK, (u + 1) * BANK, out[:, u, :])
 
         def store_page(g, t):
-            nc.sync.dma_start(out=out1_rows[g, t], in_=page[g, t][:])
+            queue = nc.sync if (g, t) == (1, 3) else nc.gpsimd
+            queue.dma_start(out=out1_rows[g, t], in_=page[g, t][:])
 
         picked = {}
 
@@ -251,12 +257,8 @@ def tile_list_plate_thinning_features_kernel(
         def weave_x(copy, g, u, slot):
             return weave(copy, picked[g][:, :, u * BANK : (u + 1) * BANK], slot)
 
-        rounded = {}
-
-        def round_page(copy, t, c):
-            if c not in rounded:
-                rounded[c] = raw.tile([P, PACK, BANK], BF16, name="rounded", tag="raw")
-            copy(out=rounded[c][:, t, :], in_=page[1, t][:, c * BANK : (c + 1) * BANK])
+        def stage_last(copy, c):
+            copy(out=staged[1, c][:, PACK - 1, :], in_=page[1, PACK - 1][:, c * BANK : (c + 1) * BANK])
 
         def late_w1(a):
             def step():
@@ -270,8 +272,8 @@ def tile_list_plate_thinning_features_kernel(
 
         Q, HALF = S // 4, S // 2
         stage_one(0, {
-            1: [gain_put(0, t, 0, Q) for t in range(3)],
-            3: [gain_put(0, t, Q, HALF) for t in range(3)] + [gain_put(0, 3, 0, Q), gain_put(0, 3, Q, HALF)],
+            1: [early_put(t, 0, Q) for t in range(4)],
+            3: [early_put(t, Q, HALF) for t in range(4)],
             7: [gain_put(0, 0, HALF, S), late_w1(0), late_w1(1)],
         })
         pair = gained_tile(5)
@@ -290,15 +292,18 @@ def tile_list_plate_thinning_features_kernel(
                 stage_page(0, t, [c])
         vec_sb = held.tile([P, 2, PACK], F32, name="vec_sb", tag="v_sc0", align_bytes=64)
         nc.sync.dma_start(out=vec_sb[:], in_=vec.rearrange("(g p t) -> p g t", g=2, t=PACK))
+        for t in range(4):
+            store_page(0, t)
         picked[1] = big.tile([P, PACK, PICK], F32, name="picked", tag="big2")
         for t in range(2):
             get(1, t, 0, PICK)
         for c in range(4):
             plane_chunk(0, c, weave(nc.scalar.copy, staged[0, c][:], c))
-        store_plane_scales(0)
-        for t in range(4):
-            store_page(0, t)
         gain_put_late(2, 3)
+        for c in range(4):
+            for t in range(3):
+                stage_page(1, t, [c])
+        store_plane_scales(0)
         for t in range(2):
             store_page(1, t)
         for t in range(4):
@@ -310,8 +315,6 @@ def tile_list_plate_thinning_features_kernel(
         gain_put_late(3, 6)
         for t in range(3):
             apply_vec(1, t, 0, PICK)
-            for c in range(4):
-                round_page(nc.scalar.copy, t, c)
 
         y = {}
 
@@ -331,8 +334,8 @@ def tile_list_plate_thinning_features_kernel(
         def y_out(copy, n, u):
             copy(out=result[u][:, n, :], in_=y[n, u][:])
 
-        def y_store(lo, hi, u):
-            nc.sync.dma_start(out=out0_rows[:, lo:hi, u * BANK : (u + 1) * BANK], in_=result[u][:, lo:hi, :])
+        def y_store(queue, lo, hi, u):
+            queue.dma_start(out=out0_rows[:, lo:hi, u * BANK : (u + 1) * BANK], in_=result[u][:, lo:hi, :])
 
         for u in range(2):
             y_pass(0, u)
@@ -341,30 +344,32 @@ def tile_list_plate_thinning_features_kernel(
         get(1, 3, 0, HALF)
         get(1, 3, HALF, PICK)
         for c in (1, 2):
-            round_page(nc.scalar.copy, 3, c)
+            stage_last(nc.scalar.copy, c)
         apply_vec(1, 3, 0, HALF)
         x_first = weave_x(nc.scalar.copy, 1, 0, 4)
         apply_vec(1, 3, HALF, PICK)
-        plane_chunk(1, 1, weave(nc.vector.tensor_copy, rounded[1][:], 1))
+        plane_chunk(1, 1, weave(nc.vector.tensor_copy, staged[1, 1][:], 1))
         quantise(x_codes[1][0][:], x_sc[1][0][:], x_first)
         y_pass(1, 0)
         x_second = weave_x(nc.vector.tensor_copy, 1, 1, 7)
-        round_page(nc.scalar.copy, 3, 0)
-        first = weave(nc.scalar.copy, rounded[0][:], 0)
-        third = weave(nc.vector.tensor_copy, rounded[2][:], 4)
+        stage_last(nc.scalar.copy, 0)
+        first = weave(nc.scalar.copy, staged[1, 0][:], 0)
+        third = weave(nc.vector.tensor_copy, staged[1, 2][:], 4)
         quantise(x_codes[1][1][:], x_sc[1][1][:], x_second)
         y_pass(1, 1)
-        round_page(nc.vector.tensor_copy, 3, 3)
+        stage_last(nc.vector.tensor_copy, 3)
         plane_chunk(1, 2, third)
-        fourth = weave(nc.vector.tensor_copy, rounded[3][:], 3)
+        fourth = weave(nc.vector.tensor_copy, staged[1, 3][:], 3)
         plane_chunk(1, 0, first)
         plane_chunk(1, 3, fourth)
         store_plane_scales(1)
         for n in range(N // P):
             y_out(nc.scalar.copy, n, 0)
             if n % 2 == 1:
-                y_store(n - 1, n + 1, 0)
-        for n in range(N // P):
-            y_out(nc.scalar.copy if n < 2 else nc.vector.tensor_copy, n, 1)
-            if n % 2 == 1:
-                y_store(n - 1, n + 1, 1)
+                y_store(nc.scalar, n - 1, n + 1, 0)
+        for n in range(2):
+            y_out(nc.scalar.copy, n, 1)
+        y_store(nc.scalar, 0, 2, 1)
+        for n in range(2, 4):
+            y_out(nc.vector.tensor_copy, n, 1)
+            y_store(nc.sync, n, n + 1, 1)

@@ -32,7 +32,7 @@ def tile_list_plate_thinning_features_kernel(
     with ExitStack() as ctx:
         held = ctx.enter_context(tc.tile_pool(name="held", bufs=1))
         big = ctx.enter_context(tc.tile_pool(name="big", bufs=1))
-        raw = ctx.enter_context(tc.tile_pool(name="raw", bufs=4))
+        raw = ctx.enter_context(tc.tile_pool(name="raw", bufs=1))
         pages = ctx.enter_context(tc.tile_pool(name="pages", bufs=8))
         small = ctx.enter_context(tc.tile_pool(name="small", bufs=4))
         planes = ctx.enter_context(tc.tile_pool(name="planes", bufs=4))
@@ -42,8 +42,11 @@ def tile_list_plate_thinning_features_kernel(
             return lst[:, lo // LANES : hi // LANES]
 
         def weave(copy, src, slot):
-            dst = held.tile([P, BANK, PACK], BF16, name="woven", tag="slot%d" % slot, align_bytes=64)
-            copy(out=dst[:].rearrange("p (c i) t -> p c t i", i=4), in_=src.rearrange("p t (c i) -> p c t i", i=4))
+            if isinstance(slot, int):
+                dst = held.tile([P, BANK, PACK], BF16, name="woven", tag="slot%d" % slot, align_bytes=64)[:]
+            else:
+                dst = slot
+            copy(out=dst.rearrange("p (c i) t -> p c t i", i=4), in_=src.rearrange("p t (c i) -> p c t i", i=4))
             return dst
 
         def quantise(codes, scales, src):
@@ -69,8 +72,8 @@ def tile_list_plate_thinning_features_kernel(
         page_sc = [held.tile([P, T2], U8, name="page_sc%d" % g, align_bytes=64) for g in range(2)]
         wgs_sb = [held.tile([P, PACK, BANK], F32, name="wgs_sb%d" % u) for u in range(2)]
 
-        def load_rows(w, g_rows, cols):
-            dst = raw.tile([P, PACK, BANK], F32, name="raw", tag="raw")
+        def load_rows(w, g_rows, cols, room):
+            dst = raw.tile([P, PACK, BANK], F32, name="raw", tag="room%d" % room, align_bytes=64)
             nc.sync.dma_start(out=dst[:], in_=w[g_rows * PASS : (g_rows + 1) * PASS, cols].rearrange("(p i) c -> p i c", i=PACK))
             return dst
 
@@ -82,7 +85,7 @@ def tile_list_plate_thinning_features_kernel(
             page[g, t] = pages.tile([P, T2], F32, name="page")
             nc.sync.dma_start(out=page[g, t][:], in_=page0_rows[g, t])
 
-        tab_sc = raw.tile([P, 2, T], U8, name="tab_sc", tag="raw")
+        tab_sc = raw.tile([P, 2, T], U8, name="tab_sc", tag="room0", align_bytes=64)
         nc.vector.memset(tab_sc[:].rearrange("p a t -> p (a t)").bitcast(I32), 0)
         nc.gpsimd.memset(w4_sc[:].rearrange("p a t -> p (a t)").bitcast(I32), 0)
         nc.vector.memset(warm[:], 1.0)
@@ -104,7 +107,7 @@ def tile_list_plate_thinning_features_kernel(
                 nc.sync.dma_start(out=wgs_sb[u][32 * q : 32 * q + 32, :, :], in_=rows)
 
         nc.sync.dma_start(out=list_tab[:], in_=offs)
-        w1_raw = [load_rows(w1, a, slice(0, PASS)) for a in range(2)]
+        w1_raw = [load_rows(w1, a, slice(0, PASS), 1 + a) for a in range(2)]
         for q in range(4):
             nc.sync.dma_start(
                 out=tab_sc[32 * q : 32 * q + 4, :, :].bitcast(I32),
@@ -124,10 +127,10 @@ def tile_list_plate_thinning_features_kernel(
         for t in range(4):
             load_page(0, t)
         load_wgs(1)
-        w1_raw_late = [load_rows(w1, a, slice(PASS, 2 * PASS)) for a in range(2)]
+        w1_raw_late = [load_rows(w1, a, slice(PASS, 2 * PASS), (3, 1)[a]) for a in range(2)]
         load_w4(1)
         nc.sync.dma_start(out=list_get[:], in_=offs3)
-        w2_raw = [load_rows(w2, g, slice(0, N)) for g in range(2)]
+        w2_raw = [load_rows(w2, g, slice(0, N), (0, 2)[g]) for g in range(2)]
         for t in range(4):
             load_page(1, t)
 
@@ -203,8 +206,7 @@ def tile_list_plate_thinning_features_kernel(
         def gained_tile(slot):
             return held.tile([P, 2, BANK], F32, name="gained", tag="slot%d" % slot, align_bytes=64)
 
-        def gain_put_late(t, slot):
-            out = gained_tile(slot)
+        def gain_put_late(t, out):
             nc.vector.tensor_scalar(
                 out=out[:], in0=h[1][:].rearrange("p (u t j) -> p u t j", u=2, t=PACK)[:, :, t, :],
                 scalar1=gain_sb[:, 1, t : t + 1], scalar2=None, op0=MULT,
@@ -239,7 +241,10 @@ def tile_list_plate_thinning_features_kernel(
         def stage_page(g, t, chunks):
             for c in chunks:
                 if (g, c) not in staged:
-                    staged[g, c] = raw.tile([P, PACK, BANK], F32, name="staged", tag="raw")
+                    if (g, c) == (1, 3):
+                        staged[g, c] = big.tile([P, PACK, BANK], F32, name="staged", tag="big1")
+                    else:
+                        staged[g, c] = raw.tile([P, PACK, BANK], F32, name="staged", tag="room%d" % c, align_bytes=64)
                 nc.sync.dma_start(out=staged[g, c][:, t, :], in_=page[g, t][:, c * BANK : (c + 1) * BANK])
 
         def plane_chunk(g, c, grouped):
@@ -256,6 +261,19 @@ def tile_list_plate_thinning_features_kernel(
 
         def weave_x(copy, g, u, slot):
             return weave(copy, picked[g][:, :, u * BANK : (u + 1) * BANK], slot)
+
+        def weave_pair(dst, src):
+            nc.scalar.copy(
+                out=dst[:, :, 0:2].rearrange("p (c i) t -> p c t i", i=4), in_=src[:, 0:2, :].rearrange("p t (c i) -> p c t i", i=4)
+            )
+
+        def woven_tile(slot):
+            return held.tile([P, BANK, PACK], BF16, name="woven", tag="slot%d" % slot, align_bytes=64)
+
+        def x_slot(dst, t, u):
+            nc.scalar.activation(
+                out=dst[:, :, t], in_=picked[1][:, t, u * BANK : (u + 1) * BANK], func=ACT.Copy, scale=vec_sb[:, 1, t : t + 1]
+            )
 
         def stage_last(copy, c):
             copy(out=staged[1, c][:, PACK - 1, :], in_=page[1, PACK - 1][:, c * BANK : (c + 1) * BANK])
@@ -299,22 +317,33 @@ def tile_list_plate_thinning_features_kernel(
             get(1, t, 0, PICK)
         for c in range(4):
             plane_chunk(0, c, weave(nc.scalar.copy, staged[0, c][:], c))
-        gain_put_late(2, 3)
-        for c in range(4):
-            for t in range(3):
+        gain_put_late(2, gained_tile(3))
+        for c in range(3):
+            for t in range(2 if c == 0 else 3):
                 stage_page(1, t, [c])
         store_plane_scales(0)
         for t in range(2):
             store_page(1, t)
         for t in range(4):
             apply_vec(0, t, 0, PICK)
+        both = raw.tile([P, 2, BANK, PACK], BF16, name="woven", tag="room3", align_bytes=64)
         for u in range(2):
-            quantise(x_codes[0][u][:], x_sc[0][u][:], weave_x(nc.scalar.copy, 0, u, 5 + u))
+            quantise(x_codes[0][u][:], x_sc[0][u][:], weave_x(nc.scalar.copy, 0, u, both[:, u, :, :]))
+        for t in range(3):
+            stage_page(1, t, [3])
         get(1, 2, 0, PICK)
         store_page(1, 2)
-        gain_put_late(3, 6)
-        for t in range(3):
+        gain_put_late(3, raw.tile([P, 2, BANK], F32, name="gained", tag="room3", align_bytes=64))
+        x_woven = [woven_tile(4), woven_tile(7)]
+        first = woven_tile(0)
+        for t in range(2):
             apply_vec(1, t, 0, PICK)
+        for u in range(2):
+            weave_pair(x_woven[u], picked[1][:, :, u * BANK : (u + 1) * BANK])
+        weave_pair(first, staged[1, 0])
+        nc.scalar.copy(out=first[:, :, 2], in_=page[1, 2][:, 0:BANK])
+        for u in range(2):
+            x_slot(x_woven[u], 2, u)
 
         y = {}
 
@@ -345,31 +374,24 @@ def tile_list_plate_thinning_features_kernel(
         get(1, 3, HALF, PICK)
         for c in (1, 2):
             stage_last(nc.scalar.copy, c)
-        apply_vec(1, 3, 0, HALF)
-        x_first = weave_x(nc.scalar.copy, 1, 0, 4)
-        apply_vec(1, 3, HALF, PICK)
-        plane_chunk(1, 1, weave(nc.vector.tensor_copy, staged[1, 1][:], 1))
-        quantise(x_codes[1][0][:], x_sc[1][0][:], x_first)
+        for u in range(2):
+            x_slot(x_woven[u], 3, u)
+        nc.scalar.copy(out=first[:, :, 3], in_=page[1, 3][:, 0:BANK])
+        second = weave(nc.vector.tensor_copy, staged[1, 1][:], 1)
+        quantise(x_codes[1][0][:], x_sc[1][0][:], x_woven[0])
         y_pass(1, 0)
-        x_second = weave_x(nc.vector.tensor_copy, 1, 1, 7)
-        stage_last(nc.scalar.copy, 0)
-        first = weave(nc.scalar.copy, staged[1, 0][:], 0)
-        third = weave(nc.vector.tensor_copy, staged[1, 2][:], 4)
-        quantise(x_codes[1][1][:], x_sc[1][1][:], x_second)
+        plane_chunk(1, 1, second)
+        quantise(x_codes[1][1][:], x_sc[1][1][:], x_woven[1])
         y_pass(1, 1)
+        third = weave(nc.vector.tensor_copy, staged[1, 2][:], 4)
         stage_last(nc.vector.tensor_copy, 3)
-        plane_chunk(1, 2, third)
-        fourth = weave(nc.vector.tensor_copy, staged[1, 3][:], 3)
         plane_chunk(1, 0, first)
+        fourth = weave(nc.vector.tensor_copy, staged[1, 3][:], 7)
+        plane_chunk(1, 2, third)
         plane_chunk(1, 3, fourth)
         store_plane_scales(1)
-        for n in range(N // P):
-            y_out(nc.scalar.copy, n, 0)
-            if n % 2 == 1:
-                y_store(nc.scalar, n - 1, n + 1, 0)
-        for n in range(2):
-            y_out(nc.scalar.copy, n, 1)
-        y_store(nc.scalar, 0, 2, 1)
-        for n in range(2, 4):
-            y_out(nc.vector.tensor_copy, n, 1)
-            y_store(nc.sync, n, n + 1, 1)
+        for u in range(2):
+            for n in range(N // P):
+                y_out(nc.vector.tensor_copy if (u, n) == (1, 3) else nc.scalar.copy, n, u)
+                if n % 2 == 1:
+                    y_store(nc.scalar, n - 1, n + 1, u)

from contextlib import ExitStack

import concourse.mybir as mybir
from concourse.masks import make_identity

K, H, N, T, S, T2, PICK = 1024, 1024, 512, 4096, 1024, 2048, 1024
FLOPS = 2 * (2 * K * H * S + H * N * PICK)

F32 = mybir.dt.float32
BF16 = mybir.dt.bfloat16
I32 = mybir.dt.int32
U32 = mybir.dt.uint32
U16 = mybir.dt.uint16
U8 = mybir.dt.uint8
FP8X4 = mybir.dt.float8_e4m3fn_x4
FP4X4 = mybir.dt.float4_e2m1fn_x4
ACT = mybir.ActivationFunctionType
MULT = mybir.AluOpType.mult

P = 128
PACK = 4
PASS = P * PACK
BANK = 512
LANES = 16


def tile_list_plate_thinning_features_kernel(
    tc, tab_words, tab_scales, w1, w4_words, w4_scales, gain, page0, wgs, vec, w2, offs, offs2, offs3,
    out_0, out_1, out_2, out_3,
):
    nc = tc.nc
    with ExitStack() as ctx:
        held = ctx.enter_context(tc.tile_pool(name="held", bufs=1))
        big = ctx.enter_context(tc.tile_pool(name="big", bufs=1))
        raw = ctx.enter_context(tc.tile_pool(name="raw", bufs=1))
        pages = ctx.enter_context(tc.tile_pool(name="pages", bufs=8))
        small = ctx.enter_context(tc.tile_pool(name="small", bufs=4))
        planes = ctx.enter_context(tc.tile_pool(name="planes", bufs=4))
        psum = ctx.enter_context(tc.psum_pool(name="psum", bufs=8))

        def entries(lst, lo, hi):
            return lst[:, lo // LANES : hi // LANES]

        def weave(copy, src, slot):
            if isinstance(slot, int):
                dst = held.tile([P, BANK, PACK], BF16, name="woven", tag="slot%d" % slot, align_bytes=64)[:]
            else:
                dst = slot
            copy(out=dst.rearrange("p (c i) t -> p c t i", i=4), in_=src.rearrange("p t (c i) -> p c t i", i=4))
            return dst

        def quantise(codes, scales, src):
            nc.vector.quantize_mx(out=codes.bitcast(FP8X4), scales=scales, in_=src[:].rearrange("p c t -> p (c t)"))

        list_tab = held.tile([P, S // LANES], U16, name="list_tab")
        list_put = held.tile([P, S // LANES], U16, name="list_put")
        list_get = held.tile([P, PICK // LANES], U16, name="list_get")
        ident = held.tile([P, P], F32, name="ident")
        gain_sb = held.tile([P, 2, PACK], F32, name="gain_sb")
        warm = held.tile([P, 8], F32, name="warm")
        w4_codes = held.tile([P, 2, 2, 2 * PASS], U8, name="w4_codes", tag="slot2", align_bytes=64)
        w4_sc = held.tile([P, 2, H], U8, name="w4_sc", align_bytes=64)
        v_codes = [held.tile([P, S], U32, name="v_codes", tag="slot%d" % a, align_bytes=64) for a in range(2)]
        v_sc = [held.tile([P, S], U8, name="v_sc", tag="v_sc%d" % a, align_bytes=64) for a in range(2)]
        w1_pair = [held.tile([P, 2, BANK], U32, name="w1_codes", tag="slot%d" % (4 - g), align_bytes=64) for g in range(2)]
        w1_codes = [[w1_pair[g][:, a, :] for a in range(2)] for g in range(2)]
        w1_sc = [[held.tile([P, BANK], U8, name="w1_sc%d%d" % (g, a), align_bytes=64) for a in range(2)] for g in range(2)]
        w2_codes = [held.tile([P, N], U32, name="w2_codes%d" % g, align_bytes=64) for g in range(2)]
        w2_sc = [held.tile([P, N], U8, name="w2_sc%d" % g, align_bytes=64) for g in range(2)]
        x_codes = [[held.tile([P, BANK], U32, name="x_codes%d%d" % (g, u), align_bytes=64) for u in range(2)] for g in range(2)]
        x_sc = [[held.tile([P, BANK], U8, name="x_sc%d%d" % (g, u), align_bytes=64) for u in range(2)] for g in range(2)]
        page_sc = [held.tile([P, T2], U8, name="page_sc%d" % g, align_bytes=64) for g in range(2)]
        wgs_sb = [held.tile([P, PACK, BANK], F32, name="wgs_sb%d" % u) for u in range(2)]

        def load_rows(w, g_rows, cols, room):
            dst = raw.tile([P, PACK, BANK], F32, name="raw", tag="room%d" % room, align_bytes=64)
            nc.sync.dma_start(out=dst[:], in_=w[g_rows * PASS : (g_rows + 1) * PASS, cols].rearrange("(p i) c -> p i c", i=PACK))
            return dst

        page0_rows = page0.rearrange("(g p t) m -> g t p m", g=2, t=PACK)
        out1_rows = out_1.rearrange("(g p t) m -> g t p m", g=2, t=PACK)
        page = {}

        def load_page(g, t):
            page[g, t] = pages.tile([P, T2], F32, name="page")
            nc.sync.dma_start(out=page[g, t][:], in_=page0_rows[g, t])

        tab_sc = raw.tile([P, 2, T], U8, name="tab_sc", tag="room0", align_bytes=64)
        nc.vector.memset(tab_sc[:].rearrange("p a t -> p (a t)").bitcast(I32), 0)
        nc.gpsimd.memset(w4_sc[:].rearrange("p a t -> p (a t)").bitcast(I32), 0)
        nc.vector.memset(warm[:], 1.0)
        nc.scalar.activation(out=warm[:, 4:5], in_=warm[:, 0:1], func=ACT.Sqrt)

        make_identity(nc, ident[:])
        def load_table(a):
            words = big.tile([P, T], I32, name="tab", tag="big%d" % a)
            nc.sync.dma_start(out=words[:], in_=tab_words[a].rearrange("p t i -> p (t i)").bitcast(I32))
            return words

        def load_w4(g):
            cols = slice(2 * g * PASS, 2 * (g + 1) * PASS)
            nc.sync.dma_start(out=w4_codes[:, g, :, :].bitcast(I32), in_=w4_words.rearrange("a p c -> p a c")[:, :, cols].bitcast(I32))

        def load_wgs(u):
            rows = wgs.rearrange("(b t) j -> b t j", t=PACK)[:, :, u * BANK : (u + 1) * BANK]
            for q in (0, 2, 1, 3):
                nc.sync.dma_start(out=wgs_sb[u][32 * q : 32 * q + 32, :, :], in_=rows)

        nc.sync.dma_start(out=list_tab[:], in_=offs)
        w1_raw = [load_rows(w1, a, slice(0, PASS), 1 + a) for a in range(2)]
        for q in range(4):
            nc.sync.dma_start(
                out=tab_sc[32 * q : 32 * q + 4, :, :].bitcast(I32),
                in_=tab_scales[:, 4 * q : 4 * q + 4, :].rearrange("a r t -> r a t").bitcast(I32),
            )
        nc.sync.dma_start(out=gain_sb[:], in_=gain.rearrange("(g p t) -> p g t", g=2, t=PACK))
        tab = [load_table(0)]
        for q in range(4):
            nc.sync.dma_start(
                out=w4_sc[32 * q : 32 * q + 4, :, :].bitcast(I32),
                in_=w4_scales[:, 4 * q : 4 * q + 4, :].rearrange("a r c -> r a c").bitcast(I32),
            )
        nc.sync.dma_start(out=list_put[:], in_=offs2)
        load_w4(0)
        tab.append(load_table(1))
        load_wgs(0)
        for t in range(4):
            load_page(0, t)
        load_wgs(1)
        w1_raw_late = [load_rows(w1, a, slice(PASS, 2 * PASS), (3, 1)[a]) for a in range(2)]
        load_w4(1)
        nc.sync.dma_start(out=list_get[:], in_=offs3)
        w2_raw = [load_rows(w2, g, slice(0, N), (0, 2)[g]) for g in range(2)]
        for t in range(4):
            load_page(1, t)

        def gather_scales(a, lo, hi):
            nc.vector.tensor_copy(out=v_sc[a][:, lo:hi], in_=tab_sc[:, a, :].indirect(entries(list_tab, lo, hi)))

        def gather_words(a, lo, hi):
            nc.vector.tensor_copy(out=v_codes[a][:, lo:hi], in_=tab[a][:].bitcast(U32).indirect(entries(list_tab, lo, hi)))

        for a in range(2):
            grouped = weave(nc.scalar.copy, w1_raw[a][:], 5 + a)
            gather_scales(a, 0, S)
            quantise(w1_codes[0][a], w1_sc[0][a][:], grouped)
        gather_words(0, 0, S)
        gather_words(1, 0, S // 2)
        gather_words(1, S // 2, S)

        h = {}
        edges = ((0, S // 4, S // 2, S), (0, S // 2, S))

        def h_piece(g, lo, hi):
            first, last = max(e for e in edges[g] if e <= lo), min(e for e in edges[g] if e >= hi)
            return h[g][:, PACK * first : PACK * last].rearrange("p (t j) -> p t j", t=PACK)[:, :, lo - first : hi - first]

        def products(g, c):
            cols = slice(c * P, (c + 1) * P)
            across = psum.tile([P, BANK], F32, name="bank")
            along = psum.tile([P, BANK], F32, name="bank")
            for a in range(2):
                nc.tensor.matmul_mx(
                    out=across[:], lhsT=v_codes[a][:, cols].bitcast(FP8X4), lhsT_scale=v_sc[a][:, cols],
                    rhs=w4_codes[:, g, a, :].bitcast(FP4X4),
                    rhs_scale=w4_sc[:, a, g * PASS : (g + 1) * PASS], start=(a == 0), stop=(a == 1),
                )
                nc.tensor.matmul_mx(
                    out=along[:], lhsT=v_codes[a][:, cols].bitcast(FP8X4), lhsT_scale=v_sc[a][:, cols],
                    rhs=w1_codes[g][a].bitcast(FP8X4), rhs_scale=w1_sc[g][a][:], start=(a == 0), stop=(a == 1),
                )
            squares = []
            for bank in (across, along):
                sq = small.tile([P, PACK, P], F32, name="small")
                nc.scalar.activation(out=sq[:], in_=bank[:].rearrange("j (p t) -> j t p", t=PACK), func=ACT.Square)
                squares.append(sq)
            return squares

        def magnitude(g, c, squares):
            total = psum.tile([P, PACK, P], F32, name="bank")
            for t in range(PACK):
                for n, sq in enumerate(squares):
                    nc.tensor.matmul(out=total[:, t, :], lhsT=sq[:, t, :], rhs=ident[:], is_transpose=True, start=(n == 0), stop=(n == 1))
            nc.scalar.activation(out=h_piece(g, c * P, (c + 1) * P), in_=total[:], func=ACT.Sqrt, bias=1.0)

        def put(g, t, lo, hi, values, factors=None):
            if factors is None:
                factors = wgs_sb[lo // BANK][:, t, lo % BANK : lo % BANK + hi - lo]
            nc.vector.tensor_tensor(out=page[g, t][:].indirect(entries(list_put, lo, hi)), in0=values, in1=factors, op=MULT)

        early = big.tile([P, PACK, BANK], F32, name="early", tag="big1")
        for t in range(PACK):
            nc.vector.tensor_scalar(out=early[:, t, :], in0=wgs_sb[0][:, t, :], scalar1=gain_sb[:, 0, t : t + 1], scalar2=None, op0=MULT)

        def early_put(t, lo, hi):
            return lambda: put(0, t, lo, hi, h_piece(0, lo, hi)[:, t, :], early[:, t, lo:hi])

        def gain_put(g, t, lo, hi, dst=None):
            def step():
                src = h_piece(g, lo, hi)[:, t, :]
                out = src if dst is None else dst()
                nc.scalar.activation(out=out, in_=src, func=ACT.Copy, scale=gain_sb[:, g, t : t + 1])
                put(g, t, lo, hi, out)
            return step

        def gained_tile(slot):
            return held.tile([P, 2, BANK], F32, name="gained", tag="slot%d" % slot, align_bytes=64)

        def gain_put_late(t, out):
            nc.vector.tensor_scalar(
                out=out[:], in0=h[1][:].rearrange("p (u t j) -> p u t j", u=2, t=PACK)[:, :, t, :],
                scalar1=gain_sb[:, 1, t : t + 1], scalar2=None, op0=MULT,
            )
            for u in range(2):
                put(1, t, u * BANK, (u + 1) * BANK, out[:, u, :])

        def store_page(g, t):
            queue = nc.sync if (g, t) == (1, 3) else nc.gpsimd
            queue.dma_start(out=out1_rows[g, t], in_=page[g, t][:])

        picked = {}

        def get(g, t, lo, hi):
            nc.vector.tensor_copy(out=picked[g][:, t, lo:hi], in_=page[g, t][:].indirect(entries(list_get, lo, hi)))

        def apply_vec(g, t, lo, hi):
            nc.scalar.activation(out=picked[g][:, t, lo:hi], in_=picked[g][:, t, lo:hi], func=ACT.Copy, scale=vec_sb[:, g, t : t + 1])

        def stage_one(g, after):
            h[g] = big.tile([P, PACK * S], F32, name="h", tag=("big2", "big0")[g])
            pending = products(g, 0)
            for c in range(S // P):
                ahead = products(g, c + 1) if c + 1 < S // P else None
                magnitude(g, c, pending)
                pending = ahead
                for step in after.get(c, ()):
                    step()

        staged = {}

        def stage_page(g, t, chunks):
            for c in chunks:
                if (g, c) not in staged:
                    if (g, c) == (1, 3):
                        staged[g, c] = big.tile([P, PACK, BANK], F32, name="staged", tag="big1")
                    else:
                        staged[g, c] = raw.tile([P, PACK, BANK], F32, name="staged", tag="room%d" % c, align_bytes=64)
                nc.sync.dma_start(out=staged[g, c][:, t, :], in_=page[g, t][:, c * BANK : (c + 1) * BANK])

        def plane_chunk(g, c, grouped):
            codes = planes.tile([P, BANK], U32, name="page_codes", align_bytes=64)
            quantise(codes[:], page_sc[g][:, c * BANK : (c + 1) * BANK], grouped)
            nc.sync.dma_start(
                out=out_2[g].rearrange("p m t -> p (m t)")[:, c * BANK * PACK : (c + 1) * BANK * PACK].bitcast(I32),
                in_=codes[:].bitcast(I32),
            )

        def store_plane_scales(g):
            for q in range(4):
                nc.sync.dma_start(out=out_3[g, 4 * q : 4 * q + 4, :].bitcast(I32), in_=page_sc[g][32 * q : 32 * q + 4, :].bitcast(I32))

        def weave_x(copy, g, u, slot):
            return weave(copy, picked[g][:, :, u * BANK : (u + 1) * BANK], slot)

        def weave_pair(dst, src):
            nc.scalar.copy(
                out=dst[:, :, 0:2].rearrange("p (c i) t -> p c t i", i=4), in_=src[:, 0:2, :].rearrange("p t (c i) -> p c t i", i=4)
            )

        def woven_tile(slot):
            return held.tile([P, BANK, PACK], BF16, name="woven", tag="slot%d" % slot, align_bytes=64)

        def x_slot(dst, t, u):
            nc.scalar.activation(
                out=dst[:, :, t], in_=picked[1][:, t, u * BANK : (u + 1) * BANK], func=ACT.Copy, scale=vec_sb[:, 1, t : t + 1]
            )

        def stage_last(copy, c):
            copy(out=staged[1, c][:, PACK - 1, :], in_=page[1, PACK - 1][:, c * BANK : (c + 1) * BANK])

        def late_w1(a):
            def step():
                quantise(w1_codes[1][a], w1_sc[1][a][:], weave(nc.scalar.copy, w1_raw_late[a][:], 5 + a))
            return step

        def late_w2(g):
            def step():
                quantise(w2_codes[g][:], w2_sc[g][:], weave(nc.scalar.copy, w2_raw[g][:], (4, 7)[g]))
            return step

        Q, HALF = S // 4, S // 2
        stage_one(0, {
            1: [early_put(t, 0, Q) for t in range(4)],
            3: [early_put(t, Q, HALF) for t in range(4)],
            7: [gain_put(0, 0, HALF, S), late_w1(0), late_w1(1)],
        })
        pair = gained_tile(5)
        gain_put(0, 1, HALF, S, lambda: pair[:, 0, :])()
        gain_put(0, 2, HALF, S, lambda: pair[:, 1, :])()
        gain_put(0, 3, HALF, S, lambda: gained_tile(6)[:, 0, :])()
        picked[0] = big.tile([P, PACK, PICK], F32, name="picked", tag="big1")
        for t in range(4):
            get(0, t, 0, PICK)
        stage_one(1, {
            3: [gain_put(1, 0, 0, HALF), gain_put(1, 1, 0, HALF), late_w2(0), late_w2(1)],
            7: [gain_put(1, 0, HALF, S), gain_put(1, 1, HALF, S)],
        })
        for c in range(4):
            for t in range(4):
                stage_page(0, t, [c])
        vec_sb = held.tile([P, 2, PACK], F32, name="vec_sb", tag="v_sc0", align_bytes=64)
        nc.sync.dma_start(out=vec_sb[:], in_=vec.rearrange("(g p t) -> p g t", g=2, t=PACK))
        for t in range(4):
            store_page(0, t)
        picked[1] = big.tile([P, PACK, PICK], F32, name="picked", tag="big2")
        for t in range(2):
            get(1, t, 0, PICK)
        for c in range(4):
            plane_chunk(0, c, weave(nc.scalar.copy, staged[0, c][:], c))
        gain_put_late(2, gained_tile(3))
        for c in range(3):
            for t in range(2 if c == 0 else 3):
                stage_page(1, t, [c])
        store_plane_scales(0)
        for t in range(2):
            store_page(1, t)
        for t in range(4):
            apply_vec(0, t, 0, PICK)
        both = raw.tile([P, 2, BANK, PACK], BF16, name="woven", tag="room3", align_bytes=64)
        for u in range(2):
            quantise(x_codes[0][u][:], x_sc[0][u][:], weave_x(nc.scalar.copy, 0, u, both[:, u, :, :]))
        for t in range(3):
            stage_page(1, t, [3])
        get(1, 2, 0, PICK)
        store_page(1, 2)
        gain_put_late(3, raw.tile([P, 2, BANK], F32, name="gained", tag="room3", align_bytes=64))
        x_woven = [woven_tile(4), woven_tile(7)]
        first = woven_tile(0)
        for t in range(2):
            apply_vec(1, t, 0, PICK)
        for u in range(2):
            weave_pair(x_woven[u], picked[1][:, :, u * BANK : (u + 1) * BANK])
        weave_pair(first, staged[1, 0])
        nc.scalar.copy(out=first[:, :, 2], in_=page[1, 2][:, 0:BANK])
        for u in range(2):
            x_slot(x_woven[u], 2, u)

        y = {}

        def y_pass(g, u):
            for n in range(N // P):
                if g == 0:
                    y[n, u] = psum.tile([P, BANK], F32, name="bank")
                cols = slice(n * P, (n + 1) * P)
                nc.tensor.matmul_mx(
                    out=y[n, u][:], lhsT=w2_codes[g][:, cols].bitcast(FP8X4), lhsT_scale=w2_sc[g][:, cols],
                    rhs=x_codes[g][u][:].bitcast(FP8X4), rhs_scale=x_sc[g][u][:], start=(g == 0), stop=(g == 1),
                )

        out0_rows = out_0.rearrange("(n p) j -> p n j", p=P)
        result = [pages.tile([P, N // P, BANK], F32, name="page") for u in range(2)]

        def y_out(copy, n, u):
            copy(out=result[u][:, n, :], in_=y[n, u][:])

        def y_store(queue, lo, hi, u):
            queue.dma_start(out=out0_rows[:, lo:hi, u * BANK : (u + 1) * BANK], in_=result[u][:, lo:hi, :])

        for u in range(2):
            y_pass(0, u)

        store_page(1, 3)
        get(1, 3, 0, HALF)
        get(1, 3, HALF, PICK)
        for c in (1, 2):
            stage_last(nc.scalar.copy, c)
        for u in range(2):
            x_slot(x_woven[u], 3, u)
        nc.scalar.copy(out=first[:, :, 3], in_=page[1, 3][:, 0:BANK])
        second = weave(nc.vector.tensor_copy, staged[1, 1][:], 1)
        quantise(x_codes[1][0][:], x_sc[1][0][:], x_woven[0])
        y_pass(1, 0)
        plane_chunk(1, 1, second)
        quantise(x_codes[1][1][:], x_sc[1][1][:], x_woven[1])
        y_pass(1, 1)
        third = weave(nc.vector.tensor_copy, staged[1, 2][:], 4)
        stage_last(nc.vector.tensor_copy, 3)
        plane_chunk(1, 0, first)
        fourth = weave(nc.vector.tensor_copy, staged[1, 3][:], 7)
        plane_chunk(1, 2, third)
        plane_chunk(1, 3, fourth)
        store_plane_scales(1)
        for u in range(2):
            for n in range(N // P):
                y_out(nc.vector.tensor_copy if (u, n) == (1, 3) else nc.scalar.copy, n, u)
                if n % 2 == 1:
                    y_store(nc.scalar, n - 1, n + 1, u)
